import numpy as np
import ml_dtypes


def mxq(x, axis, fmt="e4m3"):
    dtype, down = {"e4m3": (ml_dtypes.float8_e4m3fn, 7), "e5m2": (ml_dtypes.float8_e5m2, 14)}[fmt]
    v = np.moveaxis(np.asarray(x, np.float32).astype(ml_dtypes.bfloat16).astype(np.float64), axis, -1)
    blocks = v.reshape(v.shape[:-1] + (-1, 32))
    amax = np.abs(blocks).max(-1, keepdims=True)
    byte = np.maximum(np.where(amax > 0, np.frexp(amax)[1] - 1 + 127, 0) - down, 1)
    scale = np.exp2(byte - 127.0)
    codes = (blocks / scale).astype(np.float32).astype(dtype).astype(np.float64)
    return np.moveaxis((codes * scale).reshape(v.shape), -1, axis)


WIDE = False


def mx_kscale(k):
    if not WIDE:
        return np.ones(k)
    levels = np.array([10, -10, 5, -5, 0])
    if k % 512:
        return np.exp2(np.random.permutation(np.resize(levels, k // 32))).repeat(32)
    a = np.empty((k // 512, 16))
    for p in range(k // 512):
        a[p, :8] = np.random.permutation(np.resize(levels, 8))
        for g in range(8):
            far = levels[np.abs(levels - a[p, g]) >= 10]
            a[p, g + 8] = far[np.random.randint(len(far))]
    return np.exp2(a.ravel()).repeat(32)


def f64(x):
    return np.asarray(x).astype(np.float64)


def striped(idx):
    return np.tile(idx.reshape(-1, 16).T, (8, 1)).astype(np.uint16)


def unstriped(offs):
    return offs[:16].T.reshape(-1).astype(np.int64)


def striped8(idx):
    return np.concatenate([x.reshape(-1, 16).T for x in idx]).astype(np.uint16)


def runs(offs, k):
    lists = np.stack([offs[16 * r : 16 * r + 16].T.reshape(-1) for r in range(8)]).astype(np.int64)
    return lists[np.arange(k) % 512 // 64]


def pack_weight(w):
    k, n = w.shape
    w = f64(np.asarray(w, np.float32).astype(ml_dtypes.bfloat16)).reshape(k // 32, 32, n)
    amax = np.abs(w).max(1)
    byte = np.clip(np.where(amax > 0, np.frexp(amax)[1] - 1 + 127 - 7, 1), 1, 254)
    scaled = (w * np.exp2(127.0 - byte)[:, None, :]).reshape(k, n).astype(np.float32)
    words = np.ascontiguousarray(scaled.reshape(k // 512, 128, 4, n).transpose(0, 1, 3, 2)).astype(ml_dtypes.float8_e4m3fn).view(np.uint8)
    return words, np.ascontiguousarray(byte.astype(np.uint8).reshape(k // 512, 16, n))


def unpack_weight(words, scales):
    g, p, n, _ = words.shape
    vals = np.ascontiguousarray(words).view(ml_dtypes.float8_e4m3fn).astype(np.float64) * np.repeat(np.exp2(scales.astype(np.float64) - 127.0), 8, axis=1)[..., None]
    return vals.transpose(0, 1, 3, 2).reshape(g * 512, n)


K, T, S, H = 512, 2048, 512, 512


def setup_inputs():
    n = np.random.standard_normal
    s = mx_kscale(K)[:, None]
    u = mx_kscale(S)
    packed_xT = pack_weight(n((K, T)) * s)
    return {
        "x_words": packed_xT[0],
        "x_scales": packed_xT[1],
        "wa": (n((K, H)) / np.sqrt(K) / s).astype(np.float32),
        "wb": (n((K, H)) / np.sqrt(K) / s).astype(np.float32),
        "gt": (np.random.uniform(0.5, 1.5, (S, 1)) * u[:, None]).astype(np.float32),
        "gi": (np.random.uniform(0.5, 1.5, (S, 1)) / u[:, None]).astype(np.float32),
        "offs": striped(np.random.permutation(T)[:S]),
        "two": striped(np.random.permutation(T)[:S]),
        "n1": striped8(np.stack([np.random.permutation(H) for _ in range(8)])),
        "n2": striped8(np.stack([np.random.permutation(H) for _ in range(8)])),
        "n3": striped(np.random.permutation(H)),
        "n4": striped(np.random.permutation(H)),
    }


def reference(x_words, x_scales, wa, wb, gt, gi, offs, two, n1, n2, n3, n4):
    xq = unpack_weight(x_words, x_scales)[:, unstriped(offs)]
    a = xq.T @ mxq(f64(wa), 0, "e4m3")
    x_two = unpack_weight(x_words, x_scales)[:, unstriped(two)]
    b = x_two.T @ mxq(f64(wb), 0, "e4m3")
    z = f64(gt) * (a * (np.tanh(b[np.arange(S)[:, None], runs(n1, S)] - (b[np.arange(S)[:, None], runs(n2, S)]))))
    z2 = f64(gi) * b
    cv = 0.0625 * ((mxq(z, 0, "e4m3").T @ mxq(z2, 0, "e4m3")))
    st = cv - cv[:, unstriped(n3)]
    return np.maximum(st, st[:, unstriped(n4)])

@@ -1,0 +1,248 @@
+from contextlib import ExitStack
+
+import concourse.mybir as mybir
+from concourse.masks import make_identity
+
+K, T, S, H = 512, 2048, 512, 512
+FLOPS = 3 * 2 * 512 * 512 * 512
+
+F32 = mybir.dt.float32
+BF16 = mybir.dt.bfloat16
+I32 = mybir.dt.int32
+U32 = mybir.dt.uint32
+U16 = mybir.dt.uint16
+U8 = mybir.dt.uint8
+FP8X4 = mybir.dt.float8_e4m3fn_x4
+ALU = mybir.AluOpType
+ACT = mybir.ActivationFunctionType
+
+P = 128
+PACK = 4
+HALF = H // 2
+SPARE = 16
+LCOLS = S // 16
+
+
+def woven(dst, src):
+    return (dst.rearrange("p (c i) t -> p c t i", i=4), src.rearrange("p t (c i) -> p c t i", i=4))
+
+
+def tile_picked_momtjointbhopmx_none_p_kernel(tc, x_words, x_scales, wa, wb, gt, gi, offs, two, n1, n2, n3, n4, out):
+    nc = tc.nc
+    with ExitStack() as ctx:
+        keep = ctx.enter_context(tc.tile_pool(name="keep", bufs=1))
+        psum = ctx.enter_context(tc.psum_pool(name="psum", bufs=1))
+
+        def sb(name, shape, dtype):
+            return keep.tile(shape, dtype, name=name, align_bytes=64)
+
+        def bank(tag, name):
+            return psum.tile([P, H], F32, name=name, tag=tag)
+
+        def load_list(name, src):
+            tile = keep.tile([P, LCOLS], U16, name=name)
+            nc.sync.dma_start(tile[:], src)
+            return tile
+
+        def load_weight_half(name, w, h):
+            raw = sb(name, [P, PACK, HALF], F32)
+            nc.sync.dma_start(raw[:], w.rearrange("(p j) c -> p j c", j=PACK)[:, :, h * HALF : (h + 1) * HALF])
+            return raw
+
+        xs = sb("xs", [P, T], U8)
+        nc.vector.memset(xs[:].bitcast(I32), 0)
+        two_l = load_list("two_l", two)
+        offs_l = load_list("offs_l", offs)
+        xw = sb("xw", [P, T], I32)
+        nc.sync.dma_start(xw[:], x_words[0].rearrange("p n t -> p (n t)").bitcast(I32))
+        for q in range(4):
+            nc.scalar.dma_start(xs[32 * q : 32 * q + 4, :].bitcast(I32), x_scales[0, 4 * q : 4 * q + 4, :].bitcast(I32))
+        wb_raw = [load_weight_half("wb_raw%d" % h, wb, h) for h in range(2)]
+        n1_l = load_list("n1_l", n1)
+        n2_l = load_list("n2_l", n2)
+        wa_raw = [load_weight_half("wa_raw%d" % h, wa, h) for h in range(2)]
+        n3_l = load_list("n3_l", n3)
+        n4_l = load_list("n4_l", n4)
+
+        g_rows = sb("g_rows", [P, P], F32)
+        nc.gpsimd.memset(g_rows[:], 0.0)
+        ident = sb("ident", [P, P], F32)
+        make_identity(nc, ident[:])
+        for r, g in enumerate((gt, gi)):
+            nc.scalar.dma_start(
+                g_rows[PACK * r : PACK * (r + 1), :].rearrange("t (b e) -> t b e", e=8),
+                g.rearrange("(b t e) o -> t b (e o)", t=PACK, e=8),
+            )
+        cv_win = [sb("cv_win%d" % m, [P, H + SPARE], F32) for m in range(4)]
+        st_win = [sb("st_win%d" % m, [P, H + SPARE], F32) for m in range(4)]
+        for w in cv_win + st_win:
+            nc.gpsimd.memset(w[:, H:], 0.0)
+
+        def pick(name, lst):
+            sc = sb(name + "_sc", [P, S], U8)
+            nc.vector.tensor_copy(sc[:], xs[:].indirect(lst[:]))
+            dealt = sb(name + "_dealt", [P, S], U8)
+            nc.vector.tensor_copy(
+                dealt[:].bitcast(I32).rearrange("p (t b e) -> p b t e", t=PACK, e=2),
+                sc[:].bitcast(I32).rearrange("p (b t e) -> p b t e", t=PACK, e=2),
+            )
+            words = sb(name + "_words", [P, S], U32)
+            nc.vector.tensor_copy(
+                words[:].rearrange("p (t b e) -> p b t e", t=PACK, e=8),
+                xw[:].bitcast(U32).indirect(lst[:]),
+            )
+            return words, dealt
+
+        def cast_weight(name, raw):
+            grouped = sb(name, [P, HALF, PACK], BF16)
+            dst, src = woven(grouped[:], raw[:])
+            nc.scalar.copy(dst, src)
+            return grouped
+
+        def quantize(name, grouped, width):
+            codes = sb(name + "_codes", [P, width], U32)
+            scales = sb(name + "_scales", [P, width], U8)
+            nc.vector.quantize_mx(out=codes[:].bitcast(FP8X4), scales=scales[:], in_=grouped[:].rearrange("p c t -> p (c t)"))
+            return codes, scales
+
+        def product(dst, lhs, cols, rhs):
+            nc.tensor.matmul_mx(
+                out=dst,
+                lhsT=lhs[0][:, cols].bitcast(FP8X4),
+                lhsT_scale=lhs[1][:, cols],
+                rhs=rhs[0][:].bitcast(FP8X4),
+                rhs_scale=rhs[1][:],
+                start=True,
+                stop=True,
+            )
+
+        def half(h):
+            return slice(h * HALF, (h + 1) * HALF)
+
+        def block(t):
+            return slice(t * P, (t + 1) * P)
+
+        def list_half(lst, h):
+            return lst[:, h * (LCOLS // 2) : (h + 1) * (LCOLS // 2)]
+
+        x_two = pick("two", two_l)
+        b_bank = [bank("bank%d" % t, "b_bank%d" % t) for t in range(4)]
+        for h in range(2):
+            wb_q = quantize("wb%d" % h, cast_weight("wb_bf%d" % h, wb_raw[h]), HALF)
+            for t in range(4):
+                product(b_bank[t][:, half(h)], x_two, block(t), wb_q)
+        x_offs = pick("offs", offs_l)
+
+        g_bank = bank("bank7", "g_bank")
+        nc.tensor.transpose(g_bank[:, 0:P], g_rows[:], ident[:])
+        g_cols = sb("g_cols", [P, 2 * PACK], F32)
+        nc.vector.tensor_copy(g_cols[:], g_bank[:, 0 : 2 * PACK])
+
+        def a_half(h):
+            wa_q = quantize("wa%d" % h, cast_weight("wa_bf%d" % h, wa_raw[h]), HALF)
+            banks = [bank("bank%d" % (4 + 2 * h + u), "a_bank%d_%d" % (h, u)) for u in range(2)]
+            for t in range(4):
+                product(banks[t // 2][:, half(t % 2)], x_offs, block(t), wa_q)
+            return banks
+
+        b_win = [sb("b_win%d" % t, [P, H], F32) for t in range(4)]
+        g1 = [sb("g1_%d" % h, [P, PACK, HALF], F32) for h in range(2)]
+        dif = [sb("dif%d" % h, [P, PACK, HALF], F32) for h in range(2)]
+        th = [sb("th%d" % h, [P, PACK, HALF], F32) for h in range(2)]
+        z_rows = [sb("z_rows%d" % h, [P, PACK, HALF], BF16) for h in range(2)]
+        z2_rows = sb("z2_rows", [P, PACK, H], BF16)
+
+        def fetch1(h, t):
+            nc.scalar.activation(g1[h][:, t, :], b_win[t][:].indirect(list_half(n1_l, h)), ACT.Copy)
+
+        def fetch2(h, t):
+            nc.vector.tensor_tensor(dif[h][:, t, :], b_win[t][:].indirect(list_half(n2_l, h)), g1[h][:, t, :], ALU.subtract)
+
+        def tanh_pair(h, u):
+            nc.scalar.activation(th[h][:, 2 * u : 2 * u + 2, :], dif[h][:, 2 * u : 2 * u + 2, :], ACT.Tanh, scale=-1.0)
+
+        def z_row(h, t, banks):
+            nc.vector.scalar_tensor_tensor(
+                z_rows[h][:, t, :], banks[t // 2][:, half(t % 2)], g_cols[:, t : t + 1], th[h][:, t, :], ALU.mult, ALU.mult
+            )
+
+        def weave(name, rows, width):
+            grouped = sb(name, [P, width, PACK], BF16)
+            dst, src = woven(grouped[:], rows)
+            nc.vector.tensor_copy(dst, src)
+            return grouped
+
+        a0 = a_half(0)
+        for t in range(2):
+            nc.vector.tensor_copy(b_win[t][:], b_bank[t][:])
+            fetch1(0, t)
+        for t in range(2, 4):
+            nc.scalar.copy(b_win[t][:], b_bank[t][:])
+            fetch1(0, t)
+        for t in range(4):
+            fetch2(0, t)
+            nc.vector.tensor_scalar(z2_rows[:, t, :], b_win[t][:], g_cols[:, PACK + t : PACK + t + 1], None, ALU.mult)
+            if t % 2 == 1:
+                tanh_pair(0, t // 2)
+        for t in range(4):
+            fetch1(1, t)
+        z2_bf = weave("z2_bf", z2_rows[:], H)
+        for t in range(4):
+            z_row(0, t, a0)
+        z2_q = quantize("z2", z2_bf, H)
+        a1 = a_half(1)
+
+        cv_bank = {}
+
+        def moments(h):
+            grouped = [weave("z_bf%d" % (2 * h + u), z_rows[h][:, :, block(u)], P) for u in range(2)]
+            for u in range(2):
+                m = 2 * h + u
+                z_q = quantize("zblock%d" % m, grouped[u], P)
+                cv_bank[m] = bank("bank%d" % m, "cv_bank%d" % m)
+                product(cv_bank[m][:], z_q, slice(0, P), z2_q)
+
+        g3 = [sb("g3_%d" % m, [P, H], F32) for m in range(4)]
+        g4 = [sb("g4_%d" % m, [P, H], F32) for m in range(4)]
+        res = [sb("res%d" % m, [P, H], F32) for m in range(4)]
+
+        def fetch3(m):
+            nc.scalar.activation(cv_win[m][:, 0:H], cv_bank[m][:], ACT.Copy, scale=0.0625)
+            nc.scalar.activation(g3[m][:], cv_win[m][:].indirect(n3_l[:]), ACT.Copy)
+
+        def diff3(m):
+            nc.vector.tensor_tensor(st_win[m][:, 0:H], cv_win[m][:, 0:H], g3[m][:], ALU.subtract)
+
+        def fetch4(m):
+            nc.scalar.activation(g4[m][:], st_win[m][:].indirect(n4_l[:]), ACT.Copy)
+
+        def finish(m, cols):
+            nc.vector.tensor_tensor(res[m][:, cols], st_win[m][:, cols], g4[m][:, cols], ALU.max)
+            nc.sync.dma_start(out[block(m), cols], res[m][:, cols])
+
+        moments(0)
+        for t in range(4):
+            fetch2(1, t)
+            if t % 2 == 1:
+                tanh_pair(1, t // 2)
+                fetch3(t // 2)
+        for t in range(4):
+            z_row(1, t, a1)
+        diff3(0)
+        moments(1)
+        diff3(1)
+        fetch4(0)
+        fetch3(2)
+        finish(0, slice(0, H))
+        fetch3(3)
+        diff3(2)
+        nc.vector.tensor_copy(g4[1][:, half(0)], st_win[1][:].indirect(list_half(n4_l, 0)))
+        nc.vector.tensor_copy(g4[1][:, half(1)], st_win[1][:].indirect(list_half(n4_l, 1)))
+        finish(1, slice(0, H))
+        fetch4(2)
+        diff3(3)
+        finish(2, slice(0, H))
+        nc.scalar.activation(g4[3][:, half(1)], st_win[3][:].indirect(list_half(n4_l, 1)), ACT.Copy)
+        nc.vector.tensor_copy(g4[3][:, half(0)], st_win[3][:].indirect(list_half(n4_l, 0)))
+        finish(3, half(0))
+        finish(3, half(1))

@@ -20,7 +20,9 @@ P = 128
 PACK = 4
 HALF = H // 2
 SPARE = 16
+ST_SPARE = 192
 LCOLS = S // 16
+CHUNKS = ((0, 256), (256, 512))
 
 
 def woven(dst, src):
@@ -50,35 +52,47 @@ def tile_picked_momtjointbhopmx_none_p_kernel(tc, x_words, x_scales, wa, wb, gt,
             return raw
 
         xs = sb("xs", [P, T], U8)
-        nc.vector.memset(xs[:].bitcast(I32), 0)
+        nc.gpsimd.memset(xs[:, 0 : T // 2].bitcast(I32), 0)
+        nc.vector.memset(xs[:, T // 2 : T].bitcast(I32), 0)
         two_l = load_list("two_l", two)
         offs_l = load_list("offs_l", offs)
+        for q in range(4):
+            nc.sync.dma_start(xs[32 * q : 32 * q + 4, :].bitcast(I32), x_scales[0, 4 * q : 4 * q + 4, :].bitcast(I32))
+        wb_raw = sb("wb_raw", [P, PACK, H], F32)
+        nc.sync.dma_start(wb_raw[:], wb.rearrange("(p j) c -> p j c", j=PACK))
         xw = sb("xw", [P, T], I32)
         nc.sync.dma_start(xw[:], x_words[0].rearrange("p n t -> p (n t)").bitcast(I32))
-        for q in range(4):
-            nc.scalar.dma_start(xs[32 * q : 32 * q + 4, :].bitcast(I32), x_scales[0, 4 * q : 4 * q + 4, :].bitcast(I32))
-        wb_raw = [load_weight_half("wb_raw%d" % h, wb, h) for h in range(2)]
+        wa_raw = [load_weight_half("wa_raw0", wa, 0)]
         n1_l = load_list("n1_l", n1)
         n2_l = load_list("n2_l", n2)
-        wa_raw = [load_weight_half("wa_raw%d" % h, wa, h) for h in range(2)]
-        n3_l = load_list("n3_l", n3)
-        n4_l = load_list("n4_l", n4)
-
         g_rows = sb("g_rows", [P, P], F32)
         nc.gpsimd.memset(g_rows[:], 0.0)
         ident = sb("ident", [P, P], F32)
         make_identity(nc, ident[:])
         for r, g in enumerate((gt, gi)):
-            nc.scalar.dma_start(
+            nc.sync.dma_start(
                 g_rows[PACK * r : PACK * (r + 1), :].rearrange("t (b e) -> t b e", e=8),
                 g.rearrange("(b t e) o -> t b (e o)", t=PACK, e=8),
             )
-        cv_win = [sb("cv_win%d" % m, [P, H + SPARE], F32) for m in range(4)]
-        st_win = [sb("st_win%d" % m, [P, H + SPARE], F32) for m in range(4)]
-        for w in cv_win + st_win:
-            nc.gpsimd.memset(w[:, H:], 0.0)
+        wa_raw.append(load_weight_half("wa_raw1", wa, 1))
 
-        def pick(name, lst):
+        n3_l = load_list("n3_l", n3)
+        n4_l = load_list("n4_l", n4)
+        cv_win = [sb("cv_win%d" % m, [P, H + SPARE], F32) for m in range(4)]
+        st_win = [sb("st_win%d" % m, [P, H + ST_SPARE], F32) for m in range(4)]
+        for w in cv_win[1:] + st_win:
+            nc.gpsimd.memset(w[:, H:], 0.0)
+        nc.scalar.activation(cv_win[0][:, H:], cv_win[1][:, H:], ACT.Tanh)
+
+        def pick_words(name, lst):
+            words = sb(name + "_words", [P, S], U32)
+            nc.vector.tensor_copy(
+                words[:].rearrange("p (t b e) -> p b t e", t=PACK, e=8),
+                xw[:].bitcast(U32).indirect(lst[:]),
+            )
+            return words
+
+        def pick_scales(name, lst):
             sc = sb(name + "_sc", [P, S], U8)
             nc.vector.tensor_copy(sc[:], xs[:].indirect(lst[:]))
             dealt = sb(name + "_dealt", [P, S], U8)
@@ -86,17 +100,15 @@ def tile_picked_momtjointbhopmx_none_p_kernel(tc, x_words, x_scales, wa, wb, gt,
                 dealt[:].bitcast(I32).rearrange("p (t b e) -> p b t e", t=PACK, e=2),
                 sc[:].bitcast(I32).rearrange("p (b t e) -> p b t e", t=PACK, e=2),
             )
-            words = sb(name + "_words", [P, S], U32)
-            nc.vector.tensor_copy(
-                words[:].rearrange("p (t b e) -> p b t e", t=PACK, e=8),
-                xw[:].bitcast(U32).indirect(lst[:]),
-            )
-            return words, dealt
+            return dealt
 
-        def cast_weight(name, raw):
-            grouped = sb(name, [P, HALF, PACK], BF16)
-            dst, src = woven(grouped[:], raw[:])
-            nc.scalar.copy(dst, src)
+        def cast_weight(name, raw, width, engine="scalar"):
+            grouped = sb(name, [P, width, PACK], BF16)
+            dst, src = woven(grouped[:], raw)
+            if engine == "vector":
+                nc.vector.tensor_copy(dst, src)
+            else:
+                nc.scalar.copy(dst, src)
             return grouped
 
         def quantize(name, grouped, width):
@@ -110,8 +122,8 @@ def tile_picked_momtjointbhopmx_none_p_kernel(tc, x_words, x_scales, wa, wb, gt,
                 out=dst,
                 lhsT=lhs[0][:, cols].bitcast(FP8X4),
                 lhsT_scale=lhs[1][:, cols],
-                rhs=rhs[0][:].bitcast(FP8X4),
-                rhs_scale=rhs[1][:],
+                rhs=rhs[0][:, :].bitcast(FP8X4),
+                rhs_scale=rhs[1][:, :],
                 start=True,
                 stop=True,
             )
@@ -125,46 +137,74 @@ def tile_picked_momtjointbhopmx_none_p_kernel(tc, x_words, x_scales, wa, wb, gt,
         def list_half(lst, h):
             return lst[:, h * (LCOLS // 2) : (h + 1) * (LCOLS // 2)]
 
-        x_two = pick("two", two_l)
-        b_bank = [bank("bank%d" % t, "b_bank%d" % t) for t in range(4)]
+        two_scales = pick_scales("two", two_l)
+        offs_scales = pick_scales("offs", offs_l)
+        wb_q = (sb("wb_codes", [P, H], U32), sb("wb_scales", [P, H], U8))
         for h in range(2):
-            wb_q = quantize("wb%d" % h, cast_weight("wb_bf%d" % h, wb_raw[h]), HALF)
-            for t in range(4):
-                product(b_bank[t][:, half(h)], x_two, block(t), wb_q)
-        x_offs = pick("offs", offs_l)
+            grouped = cast_weight("wb_bf%d" % h, wb_raw[:, :, half(h)], HALF, ("vector", "scalar")[h])
+            nc.vector.quantize_mx(
+                out=wb_q[0][:, half(h)].bitcast(FP8X4), scales=wb_q[1][:, half(h)], in_=grouped[:].rearrange("p c t -> p (c t)")
+            )
+        x_two = (pick_words("two", two_l), two_scales)
+        b_bank = [bank("bank%d" % t, "b_bank%d" % t) for t in range(4)]
+        for t in range(4):
+            product(b_bank[t][:], x_two, block(t), wb_q)
+        x_offs = (pick_words("offs", offs_l), offs_scales)
 
-        g_bank = bank("bank7", "g_bank")
-        nc.tensor.transpose(g_bank[:, 0:P], g_rows[:], ident[:])
         g_cols = sb("g_cols", [P, 2 * PACK], F32)
-        nc.vector.tensor_copy(g_cols[:], g_bank[:, 0 : 2 * PACK])
 
-        def a_half(h):
-            wa_q = quantize("wa%d" % h, cast_weight("wa_bf%d" % h, wa_raw[h]), HALF)
-            banks = [bank("bank%d" % (4 + 2 * h + u), "a_bank%d_%d" % (h, u)) for u in range(2)]
-            for t in range(4):
-                product(banks[t // 2][:, half(t % 2)], x_offs, block(t), wa_q)
-            return banks
+        def turn_gains(engine):
+            g_bank = bank("bank7", "g_bank")
+            nc.tensor.transpose(g_bank[:, 0:P], g_rows[:], ident[:])
+            if engine == "vector":
+                nc.vector.tensor_copy(g_cols[:], g_bank[:, 0 : 2 * PACK])
+            else:
+                nc.scalar.copy(g_cols[:], g_bank[:, 0 : 2 * PACK])
 
-        b_win = [sb("b_win%d" % t, [P, H], F32) for t in range(4)]
-        g1 = [sb("g1_%d" % h, [P, PACK, HALF], F32) for h in range(2)]
-        dif = [sb("dif%d" % h, [P, PACK, HALF], F32) for h in range(2)]
-        th = [sb("th%d" % h, [P, PACK, HALF], F32) for h in range(2)]
-        z_rows = [sb("z_rows%d" % h, [P, PACK, HALF], BF16) for h in range(2)]
+        wa_q = (sb("wa_codes", [P, H], U32), sb("wa_scales", [P, H], U8))
+
+        def quantize_wa(h, grouped):
+            nc.vector.quantize_mx(
+                out=wa_q[0][:, half(h)].bitcast(FP8X4), scales=wa_q[1][:, half(h)], in_=grouped[:].rearrange("p c t -> p (c t)")
+            )
+
+        width = [c1 - c0 for c0, c1 in CHUNKS]
+        a_out = {}
+
+        def a_chunk(c):
+            per_bank = H // width[c]
+            first = 4 + CHUNKS[c][0] // P
+            cols = slice(CHUNKS[c][0], CHUNKS[c][1])
+            for u in range(PACK // per_bank):
+                acc = bank("bank%d" % (first + u), "a_bank%d_%d" % (c, u))
+                for v in range(per_bank):
+                    t = u * per_bank + v
+                    a_out[c, t] = acc[:, v * width[c] : (v + 1) * width[c]]
+                    product(a_out[c, t], x_offs, block(t), (wa_q[0][:, cols], wa_q[1][:, cols]))
+
+        b_win = [sb("b_win%d" % t, [P, 2 * H], F32) for t in range(4)]
+        for w in b_win:
+            nc.gpsimd.memset(w[:, H:], 0.0)
+        g1 = sb("g1", [P, PACK, H], F32)
+        dif = sb("dif", [P, PACK, H], F32)
+        th = [sb("th%d" % c, [P, PACK, w], F32) for c, w in enumerate(width)]
+        z_rows = [sb("z_rows%d" % c, [P, PACK, w], BF16) for c, w in enumerate(width)]
         z2_rows = sb("z2_rows", [P, PACK, H], BF16)
 
-        def fetch1(h, t):
-            nc.scalar.activation(g1[h][:, t, :], b_win[t][:].indirect(list_half(n1_l, h)), ACT.Copy)
+        def list_chunk(lst, c):
+            return lst[:, CHUNKS[c][0] // 16 : CHUNKS[c][1] // 16]
 
-        def fetch2(h, t):
-            nc.vector.tensor_tensor(dif[h][:, t, :], b_win[t][:].indirect(list_half(n2_l, h)), g1[h][:, t, :], ALU.subtract)
+        def fetch1(t):
+            nc.scalar.activation(g1[:, t, :], b_win[t][:].indirect(n1_l[:]), ACT.Copy)
 
-        def tanh_pair(h, u):
-            nc.scalar.activation(th[h][:, 2 * u : 2 * u + 2, :], dif[h][:, 2 * u : 2 * u + 2, :], ACT.Tanh, scale=-1.0)
+        def fetch2(t):
+            nc.vector.tensor_tensor(dif[:, t, :], b_win[t][:].indirect(n2_l[:]), g1[:, t, :], ALU.subtract)
 
-        def z_row(h, t, banks):
-            nc.vector.scalar_tensor_tensor(
-                z_rows[h][:, t, :], banks[t // 2][:, half(t % 2)], g_cols[:, t : t + 1], th[h][:, t, :], ALU.mult, ALU.mult
-            )
+        def tanh(c, t0, t1):
+            nc.scalar.activation(th[c][:, t0:t1, :], dif[:, t0:t1, CHUNKS[c][0] : CHUNKS[c][1]], ACT.Tanh, scale=-1.0)
+
+        def z_row(c, t):
+            nc.vector.scalar_tensor_tensor(z_rows[c][:, t, :], a_out[c, t], g_cols[:, t : t + 1], th[c][:, t, :], ALU.mult, ALU.mult)
 
         def weave(name, rows, width):
             grouped = sb(name, [P, width, PACK], BF16)
@@ -172,77 +212,138 @@ def tile_picked_momtjointbhopmx_none_p_kernel(tc, x_words, x_scales, wa, wb, gt,
             nc.vector.tensor_copy(dst, src)
             return grouped
 
-        a0 = a_half(0)
-        for t in range(2):
-            nc.vector.tensor_copy(b_win[t][:], b_bank[t][:])
-            fetch1(0, t)
-        for t in range(2, 4):
-            nc.scalar.copy(b_win[t][:], b_bank[t][:])
-            fetch1(0, t)
-        for t in range(4):
-            fetch2(0, t)
-            nc.vector.tensor_scalar(z2_rows[:, t, :], b_win[t][:], g_cols[:, PACK + t : PACK + t + 1], None, ALU.mult)
-            if t % 2 == 1:
-                tanh_pair(0, t // 2)
-        for t in range(4):
-            fetch1(1, t)
-        z2_bf = weave("z2_bf", z2_rows[:], H)
-        for t in range(4):
-            z_row(0, t, a0)
-        z2_q = quantize("z2", z2_bf, H)
-        a1 = a_half(1)
+        def z2_row(t, engine):
+            if engine == "vector":
+                nc.vector.tensor_scalar(z2_rows[:, t, :], b_win[t][:, 0:H], g_cols[:, PACK + t : PACK + t + 1], None, ALU.mult)
+            else:
+                nc.scalar.activation(z2_rows[:, t, :], b_bank[t][:], ACT.Copy, scale=g_cols[:, PACK + t : PACK + t + 1])
 
+        def empty_b(t, engine):
+            if engine == "vector":
+                nc.vector.tensor_copy(b_win[t][:, 0:H], b_bank[t][:])
+            else:
+                nc.scalar.copy(b_win[t][:, 0:H], b_bank[t][:])
+
+        z2_q = []
         cv_bank = {}
 
-        def moments(h):
-            grouped = [weave("z_bf%d" % (2 * h + u), z_rows[h][:, :, block(u)], P) for u in range(2)]
-            for u in range(2):
-                m = 2 * h + u
-                z_q = quantize("zblock%d" % m, grouped[u], P)
+        z_bf = {}
+
+        def weave_z(m):
+            c = [i for i, (c0, c1) in enumerate(CHUNKS) if c0 <= m * P < c1][0]
+            at = m * P - CHUNKS[c][0]
+            z_bf[m] = weave("z_bf%d" % m, z_rows[c][:, :, at : at + P], P)
+
+        def moment(m):
+            z_q = quantize("zblock%d" % m, z_bf[m], P)
+            cv_bank[m] = bank("bank%d" % m, "cv_bank%d" % m)
+            product(cv_bank[m][:], z_q, slice(0, P), z2_q[0])
+
+        def moment_pair(grouped):
+            z_q = quantize("zblocks23", grouped, HALF)
+            for m in (2, 3):
                 cv_bank[m] = bank("bank%d" % m, "cv_bank%d" % m)
-                product(cv_bank[m][:], z_q, slice(0, P), z2_q)
+                product(cv_bank[m][:], z_q, block(m - 2), z2_q[0])
 
         g3 = [sb("g3_%d" % m, [P, H], F32) for m in range(4)]
         g4 = [sb("g4_%d" % m, [P, H], F32) for m in range(4)]
         res = [sb("res%d" % m, [P, H], F32) for m in range(4)]
 
+        def empty_cv(m, engine):
+            if engine == "vector":
+                nc.vector.tensor_scalar(cv_win[m][:, 0:H], cv_bank[m][:], 0.0625, None, ALU.mult)
+            else:
+                nc.scalar.activation(cv_win[m][:, 0:H], cv_bank[m][:], ACT.Copy, scale=0.0625)
+
         def fetch3(m):
-            nc.scalar.activation(cv_win[m][:, 0:H], cv_bank[m][:], ACT.Copy, scale=0.0625)
             nc.scalar.activation(g3[m][:], cv_win[m][:].indirect(n3_l[:]), ACT.Copy)
 
-        def diff3(m):
-            nc.vector.tensor_tensor(st_win[m][:, 0:H], cv_win[m][:, 0:H], g3[m][:], ALU.subtract)
+        def fetch3_half(m, h):
+            nc.scalar.activation(g3[m][:, half(h)], cv_win[m][:].indirect(list_half(n3_l, h)), ACT.Copy)
 
-        def fetch4(m):
-            nc.scalar.activation(g4[m][:], st_win[m][:].indirect(n4_l[:]), ACT.Copy)
+        def diff3(m, cols):
+            nc.vector.tensor_tensor(st_win[m][:, cols], cv_win[m][:, cols], g3[m][:, cols], ALU.subtract)
+
+        def fetch4(m, engine="scalar"):
+            if engine == "vector":
+                nc.vector.tensor_copy(g4[m][:], st_win[m][:].indirect(n4_l[:]))
+            else:
+                nc.scalar.activation(g4[m][:], st_win[m][:].indirect(n4_l[:]), ACT.Copy)
+
+        def fetch4_half(engine, m, h):
+            if engine == "vector":
+                nc.vector.tensor_copy(g4[m][:, half(h)], st_win[m][:].indirect(list_half(n4_l, h)))
+            else:
+                nc.scalar.activation(g4[m][:, half(h)], st_win[m][:].indirect(list_half(n4_l, h)), ACT.Copy)
 
         def finish(m, cols):
             nc.vector.tensor_tensor(res[m][:, cols], st_win[m][:, cols], g4[m][:, cols], ALU.max)
             nc.sync.dma_start(out[block(m), cols], res[m][:, cols])
 
-        moments(0)
-        for t in range(4):
-            fetch2(1, t)
-            if t % 2 == 1:
-                tanh_pair(1, t // 2)
-                fetch3(t // 2)
-        for t in range(4):
-            z_row(1, t, a1)
-        diff3(0)
-        moments(1)
-        diff3(1)
+        whole = slice(0, H)
+        wa_bf0 = cast_weight("wa_bf0", wa_raw[0][:], HALF)
+        empty_b(0, "vector")
+        fetch1(0)
+        empty_b(1, "vector")
+        quantize_wa(0, wa_bf0)
+        fetch1(1)
+        empty_b(2, "vector")
+        turn_gains("vector")
+        a_chunk(0)
+        fetch2(0)
+        empty_b(3, "scalar")
+        fetch1(2)
+        fetch2(1)
+        fetch1(3)
+        z2_row(0, "vector")
+        z2_row(1, "vector")
+        fetch2(2)
+        tanh(0, 0, 2)
+        z2_row(2, "scalar")
+        z2_row(3, "scalar")
+        fetch2(3)
+        tanh(0, 2, 4)
+        z_row(0, 0)
+        z_row(0, 1)
+        z2_bf = weave("z2_bf", z2_rows[:], H)
+        z_row(0, 2)
+        z_row(0, 3)
+        wa_bf1 = cast_weight("wa_bf1", wa_raw[1][:], HALF)
+        quantize_wa(1, wa_bf1)
+        a_chunk(1)
+        weave_z(0)
+        z2_q.append(quantize("z2", z2_bf, H))
+        tanh(1, 0, 2)
+        tanh(1, 2, 4)
+        moment(0)
+        weave_z(1)
+        z_row(1, 0)
+        moment(1)
+        empty_cv(0, "scalar")
+        fetch3(0)
+        for t in range(1, 4):
+            z_row(1, t)
+        empty_cv(1, "vector")
+        fetch3(1)
+        weave_z(2)
+        weave_z(3)
+        moment(2)
+        moment(3)
+        diff3(0, whole)
+        empty_cv(2, "vector")
         fetch4(0)
+        diff3(1, whole)
         fetch3(2)
-        finish(0, slice(0, H))
+        empty_cv(3, "vector")
+        finish(0, whole)
         fetch3(3)
-        diff3(2)
-        nc.vector.tensor_copy(g4[1][:, half(0)], st_win[1][:].indirect(list_half(n4_l, 0)))
-        nc.vector.tensor_copy(g4[1][:, half(1)], st_win[1][:].indirect(list_half(n4_l, 1)))
-        finish(1, slice(0, H))
+        fetch4(1, "vector")
+        diff3(2, whole)
+        diff3(3, whole)
         fetch4(2)
-        diff3(3)
-        finish(2, slice(0, H))
-        nc.scalar.activation(g4[3][:, half(1)], st_win[3][:].indirect(list_half(n4_l, 1)), ACT.Copy)
-        nc.vector.tensor_copy(g4[3][:, half(0)], st_win[3][:].indirect(list_half(n4_l, 0)))
+        finish(1, whole)
+        fetch4_half("vector", 3, 0)
+        fetch4_half("scalar", 3, 1)
+        finish(2, whole)
         finish(3, half(0))
         finish(3, half(1))

@@ -78,11 +78,14 @@ def tile_picked_momtjointbhopmx_none_p_kernel(tc, x_words, x_scales, wa, wb, gt,
 
         n3_l = load_list("n3_l", n3)
         n4_l = load_list("n4_l", n4)
+        b_win = [sb("b_win%d" % t, [P, 2 * H], F32) for t in range(4)]
         cv_win = [sb("cv_win%d" % m, [P, H + SPARE], F32) for m in range(4)]
-        st_win = [sb("st_win%d" % m, [P, H + ST_SPARE], F32) for m in range(4)]
-        for w in cv_win[1:] + st_win:
-            nc.gpsimd.memset(w[:, H:], 0.0)
-        nc.scalar.activation(cv_win[0][:, H:], cv_win[1][:, H:], ACT.Tanh)
+        st_win = [sb("st_win%d" % m, [P, H + (SPARE, ST_SPARE, SPARE, 0)[m]], F32) for m in range(4)]
+        for w in b_win[0:1] + cv_win + st_win[0:3]:
+            nc.vector.memset(w[:, H:], 0.0)
+        nc.scalar.activation(b_win[1][:, H:], b_win[0][:, H:], ACT.Tanh)
+        for w in b_win[2:]:
+            nc.scalar.copy(w[:, H:], b_win[0][:, H:])
 
         def pick_words(name, lst):
             words = sb(name + "_words", [P, S], U32)
@@ -182,9 +185,6 @@ def tile_picked_momtjointbhopmx_none_p_kernel(tc, x_words, x_scales, wa, wb, gt,
                     a_out[c, t] = acc[:, v * width[c] : (v + 1) * width[c]]
                     product(a_out[c, t], x_offs, block(t), (wa_q[0][:, cols], wa_q[1][:, cols]))
 
-        b_win = [sb("b_win%d" % t, [P, 2 * H], F32) for t in range(4)]
-        for w in b_win:
-            nc.gpsimd.memset(w[:, H:], 0.0)
         g1 = sb("g1", [P, PACK, H], F32)
         dif = sb("dif", [P, PACK, H], F32)
         th = [sb("th%d" % c, [P, PACK, w], F32) for c, w in enumerate(width)]
@@ -206,10 +206,13 @@ def tile_picked_momtjointbhopmx_none_p_kernel(tc, x_words, x_scales, wa, wb, gt,
         def z_row(c, t):
             nc.vector.scalar_tensor_tensor(z_rows[c][:, t, :], a_out[c, t], g_cols[:, t : t + 1], th[c][:, t, :], ALU.mult, ALU.mult)
 
-        def weave(name, rows, width):
+        def weave(name, rows, width, engine="vector"):
             grouped = sb(name, [P, width, PACK], BF16)
             dst, src = woven(grouped[:], rows)
-            nc.vector.tensor_copy(dst, src)
+            if engine == "vector":
+                nc.vector.tensor_copy(dst, src)
+            else:
+                nc.scalar.copy(dst, src)
             return grouped
 
         def z2_row(t, engine):
@@ -229,10 +232,10 @@ def tile_picked_momtjointbhopmx_none_p_kernel(tc, x_words, x_scales, wa, wb, gt,
 
         z_bf = {}
 
-        def weave_z(m):
+        def weave_z(m, engine="vector"):
             c = [i for i, (c0, c1) in enumerate(CHUNKS) if c0 <= m * P < c1][0]
             at = m * P - CHUNKS[c][0]
-            z_bf[m] = weave("z_bf%d" % m, z_rows[c][:, :, at : at + P], P)
+            z_bf[m] = weave("z_bf%d" % m, z_rows[c][:, :, at : at + P], P, engine)
 
         def moment(m):
             z_q = quantize("zblock%d" % m, z_bf[m], P)

@@ -52,8 +52,7 @@ def tile_picked_momtjointbhopmx_none_p_kernel(tc, x_words, x_scales, wa, wb, gt,
             return raw
 
         xs = sb("xs", [P, T], U8)
-        nc.gpsimd.memset(xs[:, 0 : T // 2].bitcast(I32), 0)
-        nc.vector.memset(xs[:, T // 2 : T].bitcast(I32), 0)
+        nc.vector.memset(xs[:].bitcast(I32), 0)
         two_l = load_list("two_l", two)
         offs_l = load_list("offs_l", offs)
         for q in range(4):
@@ -66,9 +65,10 @@ def tile_picked_momtjointbhopmx_none_p_kernel(tc, x_words, x_scales, wa, wb, gt,
         n1_l = load_list("n1_l", n1)
         n2_l = load_list("n2_l", n2)
         g_rows = sb("g_rows", [P, P], F32)
-        nc.gpsimd.memset(g_rows[:], 0.0)
+        nc.vector.memset(g_rows[:], 0.0)
         ident = sb("ident", [P, P], F32)
-        make_identity(nc, ident[:])
+        nc.vector.memset(ident[:], 0.0)
+        make_identity(nc, ident[:], nomemset=True)
         for r, g in enumerate((gt, gi)):
             nc.sync.dma_start(
                 g_rows[PACK * r : PACK * (r + 1), :].rearrange("t (b e) -> t b e", e=8),
@@ -80,7 +80,7 @@ def tile_picked_momtjointbhopmx_none_p_kernel(tc, x_words, x_scales, wa, wb, gt,
         n4_l = load_list("n4_l", n4)
         b_win = [sb("b_win%d" % t, [P, 2 * H], F32) for t in range(4)]
         cv_win = [sb("cv_win%d" % m, [P, H + SPARE], F32) for m in range(4)]
-        st_win = [sb("st_win%d" % m, [P, H + (SPARE, ST_SPARE, SPARE, 0)[m]], F32) for m in range(4)]
+        st_win = [sb("st_win%d" % m, [P, H + (ST_SPARE, SPARE, SPARE, 0)[m]], F32) for m in range(4)]
         for w in b_win[0:1] + cv_win + st_win[0:3]:
             nc.vector.memset(w[:, H:], 0.0)
         nc.scalar.activation(b_win[1][:, H:], b_win[0][:, H:], ACT.Tanh)
@@ -110,6 +110,8 @@ def tile_picked_momtjointbhopmx_none_p_kernel(tc, x_words, x_scales, wa, wb, gt,
             dst, src = woven(grouped[:], raw)
             if engine == "vector":
                 nc.vector.tensor_copy(dst, src)
+            elif engine == "gpsimd":
+                nc.gpsimd.tensor_scalar(grouped[:], raw.rearrange("p t c -> p c t"), 1.0, 0.0, ALU.mult, ALU.add)
             else:
                 nc.scalar.copy(dst, src)
             return grouped
@@ -227,7 +229,13 @@ def tile_picked_momtjointbhopmx_none_p_kernel(tc, x_words, x_scales, wa, wb, gt,
             else:
                 nc.scalar.copy(b_win[t][:, 0:H], b_bank[t][:])
 
-        z2_q = []
+        z2_q = [(sb("z2_codes", [P, H], U32), sb("z2_scales", [P, H], U8))]
+
+        def quantize_z2(h, grouped):
+            nc.vector.quantize_mx(
+                out=z2_q[0][0][:, half(h)].bitcast(FP8X4), scales=z2_q[0][1][:, half(h)], in_=grouped[:].rearrange("p c t -> p (c t)")
+            )
+
         cv_bank = {}
 
         z_bf = {}
@@ -285,48 +293,39 @@ def tile_picked_momtjointbhopmx_none_p_kernel(tc, x_words, x_scales, wa, wb, gt,
 
         whole = slice(0, H)
         wa_bf0 = cast_weight("wa_bf0", wa_raw[0][:], HALF)
-        empty_b(0, "vector")
-        fetch1(0)
-        empty_b(1, "vector")
-        quantize_wa(0, wa_bf0)
-        fetch1(1)
-        empty_b(2, "vector")
+        wa_bf1 = cast_weight("wa_bf1", wa_raw[1][:], HALF, "gpsimd")
+        for t in range(4):
+            empty_b(t, "vector")
+            fetch1(t)
         turn_gains("vector")
+        quantize_wa(0, wa_bf0)
         a_chunk(0)
         fetch2(0)
-        empty_b(3, "scalar")
-        fetch1(2)
-        fetch2(1)
-        fetch1(3)
-        z2_row(0, "vector")
-        z2_row(1, "vector")
-        fetch2(2)
-        tanh(0, 0, 2)
-        z2_row(2, "scalar")
-        z2_row(3, "scalar")
-        fetch2(3)
-        tanh(0, 2, 4)
-        z_row(0, 0)
-        z_row(0, 1)
-        z2_bf = weave("z2_bf", z2_rows[:], H)
-        z_row(0, 2)
-        z_row(0, 3)
-        wa_bf1 = cast_weight("wa_bf1", wa_raw[1][:], HALF)
         quantize_wa(1, wa_bf1)
         a_chunk(1)
+        for t in range(1, 4):
+            fetch2(t)
+        for t in range(4):
+            z2_row(t, "scalar")
+        tanh(0, 0, 2)
+        tanh(0, 2, 4)
+        z2_bf0 = weave("z2_bf0", z2_rows[:, :, half(0)], HALF)
+        z2_bf1 = weave("z2_bf1", z2_rows[:, :, half(1)], HALF, "scalar")
+        for t in range(4):
+            z_row(0, t)
         weave_z(0)
-        z2_q.append(quantize("z2", z2_bf, H))
+        quantize_z2(0, z2_bf0)
+        quantize_z2(1, z2_bf1)
+        moment(0)
         tanh(1, 0, 2)
         tanh(1, 2, 4)
-        moment(0)
         weave_z(1)
-        z_row(1, 0)
+        for t in range(4):
+            z_row(1, t)
         moment(1)
         empty_cv(0, "scalar")
+        empty_cv(1, "scalar")
         fetch3(0)
-        for t in range(1, 4):
-            z_row(1, t)
-        empty_cv(1, "vector")
         fetch3(1)
         weave_z(2)
         weave_z(3)
@@ -334,14 +333,14 @@ def tile_picked_momtjointbhopmx_none_p_kernel(tc, x_words, x_scales, wa, wb, gt,
         moment(3)
         diff3(0, whole)
         empty_cv(2, "vector")
-        fetch4(0)
-        diff3(1, whole)
         fetch3(2)
         empty_cv(3, "vector")
-        finish(0, whole)
+        diff3(1, whole)
         fetch3(3)
-        fetch4(1, "vector")
+        fetch4(0, "vector")
         diff3(2, whole)
+        fetch4(1)
+        finish(0, whole)
         diff3(3, whole)
         fetch4(2)
         finish(1, whole)

from contextlib import ExitStack

import concourse.mybir as mybir
from concourse.masks import make_identity

K, T, S, H = 512, 2048, 512, 512
FLOPS = 3 * 2 * 512 * 512 * 512

F32 = mybir.dt.float32
BF16 = mybir.dt.bfloat16
I32 = mybir.dt.int32
U32 = mybir.dt.uint32
U16 = mybir.dt.uint16
U8 = mybir.dt.uint8
FP8X4 = mybir.dt.float8_e4m3fn_x4
ALU = mybir.AluOpType
ACT = mybir.ActivationFunctionType

P = 128
PACK = 4
HALF = H // 2
SPARE = 16
ST_SPARE = 192
LCOLS = S // 16
CHUNKS = ((0, 256), (256, 512))


def woven(dst, src):
    return (dst.rearrange("p (c i) t -> p c t i", i=4), src.rearrange("p t (c i) -> p c t i", i=4))


def tile_picked_momtjointbhopmx_none_p_kernel(tc, x_words, x_scales, wa, wb, gt, gi, offs, two, n1, n2, n3, n4, out):
    nc = tc.nc
    with ExitStack() as ctx:
        keep = ctx.enter_context(tc.tile_pool(name="keep", bufs=1))
        psum = ctx.enter_context(tc.psum_pool(name="psum", bufs=1))

        def sb(name, shape, dtype):
            return keep.tile(shape, dtype, name=name, align_bytes=64)

        def bank(tag, name):
            return psum.tile([P, H], F32, name=name, tag=tag)

        def load_list(name, src):
            tile = keep.tile([P, LCOLS], U16, name=name)
            nc.sync.dma_start(tile[:], src)
            return tile

        def load_weight_half(name, w, h):
            raw = sb(name, [P, PACK, HALF], F32)
            nc.sync.dma_start(raw[:], w.rearrange("(p j) c -> p j c", j=PACK)[:, :, h * HALF : (h + 1) * HALF])
            return raw

        xs = sb("xs", [P, T], U8)
        nc.vector.memset(xs[:].bitcast(I32), 0)
        two_l = load_list("two_l", two)
        offs_l = load_list("offs_l", offs)
        for q in range(4):
            nc.sync.dma_start(xs[32 * q : 32 * q + 4, :].bitcast(I32), x_scales[0, 4 * q : 4 * q + 4, :].bitcast(I32))
        wb_raw = sb("wb_raw", [P, PACK, H], F32)
        nc.sync.dma_start(wb_raw[:], wb.rearrange("(p j) c -> p j c", j=PACK))
        xw = sb("xw", [P, T], I32)
        nc.sync.dma_start(xw[:], x_words[0].rearrange("p n t -> p (n t)").bitcast(I32))
        wa_raw = [load_weight_half("wa_raw0", wa, 0)]
        n1_l = load_list("n1_l", n1)
        n2_l = load_list("n2_l", n2)
        g_rows = sb("g_rows", [P, P], F32)
        nc.vector.memset(g_rows[:], 0.0)
        ident = sb("ident", [P, P], F32)
        nc.vector.memset(ident[:], 0.0)
        make_identity(nc, ident[:], nomemset=True)
        for r, g in enumerate((gt, gi)):
            nc.sync.dma_start(
                g_rows[PACK * r : PACK * (r + 1), :].rearrange("t (b e) -> t b e", e=8),
                g.rearrange("(b t e) o -> t b (e o)", t=PACK, e=8),
            )
        wa_raw.append(load_weight_half("wa_raw1", wa, 1))

        n3_l = load_list("n3_l", n3)
        n4_l = load_list("n4_l", n4)
        b_win = [sb("b_win%d" % t, [P, 2 * H], F32) for t in range(4)]
        cv_win = [sb("cv_win%d" % m, [P, H + SPARE], F32) for m in range(4)]
        st_win = [sb("st_win%d" % m, [P, H + (ST_SPARE, SPARE, SPARE, 0)[m]], F32) for m in range(4)]
        for w in b_win[0:1] + cv_win + st_win[0:3]:
            nc.vector.memset(w[:, H:], 0.0)
        nc.scalar.activation(b_win[1][:, H:], b_win[0][:, H:], ACT.Tanh)
        for w in b_win[2:]:
            nc.scalar.copy(w[:, H:], b_win[0][:, H:])

        def pick_words(name, lst):
            words = sb(name + "_words", [P, S], U32)
            nc.vector.tensor_copy(
                words[:].rearrange("p (t b e) -> p b t e", t=PACK, e=8),
                xw[:].bitcast(U32).indirect(lst[:]),
            )
            return words

        def pick_scales(name, lst):
            sc = sb(name + "_sc", [P, S], U8)
            nc.vector.tensor_copy(sc[:], xs[:].indirect(lst[:]))
            dealt = sb(name + "_dealt", [P, S], U8)
            nc.vector.tensor_copy(
                dealt[:].bitcast(I32).rearrange("p (t b e) -> p b t e", t=PACK, e=2),
                sc[:].bitcast(I32).rearrange("p (b t e) -> p b t e", t=PACK, e=2),
            )
            return dealt

        def cast_weight(name, raw, width, engine="scalar"):
            grouped = sb(name, [P, width, PACK], BF16)
            dst, src = woven(grouped[:], raw)
            if engine == "vector":
                nc.vector.tensor_copy(dst, src)
            elif engine == "gpsimd":
                nc.gpsimd.tensor_scalar(grouped[:], raw.rearrange("p t c -> p c t"), 1.0, 0.0, ALU.mult, ALU.add)
            else:
                nc.scalar.copy(dst, src)
            return grouped

        def quantize(name, grouped, width):
            codes = sb(name + "_codes", [P, width], U32)
            scales = sb(name + "_scales", [P, width], U8)
            nc.vector.quantize_mx(out=codes[:].bitcast(FP8X4), scales=scales[:], in_=grouped[:].rearrange("p c t -> p (c t)"))
            return codes, scales

        def product(dst, lhs, cols, rhs):
            nc.tensor.matmul_mx(
                out=dst,
                lhsT=lhs[0][:, cols].bitcast(FP8X4),
                lhsT_scale=lhs[1][:, cols],
                rhs=rhs[0][:, :].bitcast(FP8X4),
                rhs_scale=rhs[1][:, :],
                start=True,
                stop=True,
            )

        def half(h):
            return slice(h * HALF, (h + 1) * HALF)

        def block(t):
            return slice(t * P, (t + 1) * P)

        def list_half(lst, h):
            return lst[:, h * (LCOLS // 2) : (h + 1) * (LCOLS // 2)]

        two_scales = pick_scales("two", two_l)
        offs_scales = pick_scales("offs", offs_l)
        wb_q = (sb("wb_codes", [P, H], U32), sb("wb_scales", [P, H], U8))
        for h in range(2):
            grouped = cast_weight("wb_bf%d" % h, wb_raw[:, :, half(h)], HALF, ("vector", "scalar")[h])
            nc.vector.quantize_mx(
                out=wb_q[0][:, half(h)].bitcast(FP8X4), scales=wb_q[1][:, half(h)], in_=grouped[:].rearrange("p c t -> p (c t)")
            )
        x_two = (pick_words("two", two_l), two_scales)
        b_bank = [bank("bank%d" % t, "b_bank%d" % t) for t in range(4)]
        for t in range(4):
            product(b_bank[t][:], x_two, block(t), wb_q)
        x_offs = (pick_words("offs", offs_l), offs_scales)

        g_cols = sb("g_cols", [P, 2 * PACK], F32)

        def turn_gains(engine):
            g_bank = bank("bank7", "g_bank")
            nc.tensor.transpose(g_bank[:, 0:P], g_rows[:], ident[:])
            if engine == "vector":
                nc.vector.tensor_copy(g_cols[:], g_bank[:, 0 : 2 * PACK])
            else:
                nc.scalar.copy(g_cols[:], g_bank[:, 0 : 2 * PACK])

        wa_q = (sb("wa_codes", [P, H], U32), sb("wa_scales", [P, H], U8))

        def quantize_wa(h, grouped):
            nc.vector.quantize_mx(
                out=wa_q[0][:, half(h)].bitcast(FP8X4), scales=wa_q[1][:, half(h)], in_=grouped[:].rearrange("p c t -> p (c t)")
            )

        width = [c1 - c0 for c0, c1 in CHUNKS]
        a_out = {}

        def a_chunk(c):
            per_bank = H // width[c]
            first = 4 + CHUNKS[c][0] // P
            cols = slice(CHUNKS[c][0], CHUNKS[c][1])
            for u in range(PACK // per_bank):
                acc = bank("bank%d" % (first + u), "a_bank%d_%d" % (c, u))
                for v in range(per_bank):
                    t = u * per_bank + v
                    a_out[c, t] = acc[:, v * width[c] : (v + 1) * width[c]]
                    product(a_out[c, t], x_offs, block(t), (wa_q[0][:, cols], wa_q[1][:, cols]))

        g1 = sb("g1", [P, PACK, H], F32)
        dif = sb("dif", [P, PACK, H], F32)
        th = [sb("th%d" % c, [P, PACK, w], F32) for c, w in enumerate(width)]
        z_rows = [sb("z_rows%d" % c, [P, PACK, w], BF16) for c, w in enumerate(width)]
        z2_rows = sb("z2_rows", [P, PACK, H], BF16)

        def list_chunk(lst, c):
            return lst[:, CHUNKS[c][0] // 16 : CHUNKS[c][1] // 16]

        def fetch1(t):
            nc.scalar.activation(g1[:, t, :], b_win[t][:].indirect(n1_l[:]), ACT.Copy)

        def fetch2(t):
            nc.vector.tensor_tensor(dif[:, t, :], b_win[t][:].indirect(n2_l[:]), g1[:, t, :], ALU.subtract)

        def tanh(c, t0, t1):
            nc.scalar.activation(th[c][:, t0:t1, :], dif[:, t0:t1, CHUNKS[c][0] : CHUNKS[c][1]], ACT.Tanh, scale=-1.0)

        def z_row(c, t):
            nc.vector.scalar_tensor_tensor(z_rows[c][:, t, :], a_out[c, t], g_cols[:, t : t + 1], th[c][:, t, :], ALU.mult, ALU.mult)

        def weave(name, rows, width, engine="vector"):
            grouped = sb(name, [P, width, PACK], BF16)
            dst, src = woven(grouped[:], rows)
            if engine == "vector":
                nc.vector.tensor_copy(dst, src)
            else:
                nc.scalar.copy(dst, src)
            return grouped

        def z2_row(t, engine):
            if engine == "vector":
                nc.vector.tensor_scalar(z2_rows[:, t, :], b_win[t][:, 0:H], g_cols[:, PACK + t : PACK + t + 1], None, ALU.mult)
            else:
                nc.scalar.activation(z2_rows[:, t, :], b_bank[t][:], ACT.Copy, scale=g_cols[:, PACK + t : PACK + t + 1])

        def empty_b(t, engine):
            if engine == "vector":
                nc.vector.tensor_copy(b_win[t][:, 0:H], b_bank[t][:])
            else:
                nc.scalar.copy(b_win[t][:, 0:H], b_bank[t][:])

        z2_q = [(sb("z2_codes", [P, H], U32), sb("z2_scales", [P, H], U8))]

        def quantize_z2(h, grouped):
            nc.vector.quantize_mx(
                out=z2_q[0][0][:, half(h)].bitcast(FP8X4), scales=z2_q[0][1][:, half(h)], in_=grouped[:].rearrange("p c t -> p (c t)")
            )

        cv_bank = {}

        z_bf = {}

        def weave_z(m, engine="vector"):
            c = [i for i, (c0, c1) in enumerate(CHUNKS) if c0 <= m * P < c1][0]
            at = m * P - CHUNKS[c][0]
            z_bf[m] = weave("z_bf%d" % m, z_rows[c][:, :, at : at + P], P, engine)

        def moment(m):
            z_q = quantize("zblock%d" % m, z_bf[m], P)
            cv_bank[m] = bank("bank%d" % m, "cv_bank%d" % m)
            product(cv_bank[m][:], z_q, slice(0, P), z2_q[0])

        def moment_pair(grouped):
            z_q = quantize("zblocks23", grouped, HALF)
            for m in (2, 3):
                cv_bank[m] = bank("bank%d" % m, "cv_bank%d" % m)
                product(cv_bank[m][:], z_q, block(m - 2), z2_q[0])

        g3 = [sb("g3_%d" % m, [P, H], F32) for m in range(4)]
        g4 = [sb("g4_%d" % m, [P, H], F32) for m in range(4)]
        res = [sb("res%d" % m, [P, H], F32) for m in range(4)]

        def empty_cv(m, engine):
            if engine == "vector":
                nc.vector.tensor_scalar(cv_win[m][:, 0:H], cv_bank[m][:], 0.0625, None, ALU.mult)
            else:
                nc.scalar.activation(cv_win[m][:, 0:H], cv_bank[m][:], ACT.Copy, scale=0.0625)

        def fetch3(m):
            nc.scalar.activation(g3[m][:], cv_win[m][:].indirect(n3_l[:]), ACT.Copy)

        def fetch3_half(m, h):
            nc.scalar.activation(g3[m][:, half(h)], cv_win[m][:].indirect(list_half(n3_l, h)), ACT.Copy)

        def diff3(m, cols):
            nc.vector.tensor_tensor(st_win[m][:, cols], cv_win[m][:, cols], g3[m][:, cols], ALU.subtract)

        def fetch4(m, engine="scalar"):
            if engine == "vector":
                nc.vector.tensor_copy(g4[m][:], st_win[m][:].indirect(n4_l[:]))
            else:
                nc.scalar.activation(g4[m][:], st_win[m][:].indirect(n4_l[:]), ACT.Copy)

        def fetch4_half(engine, m, h):
            if engine == "vector":
                nc.vector.tensor_copy(g4[m][:, half(h)], st_win[m][:].indirect(list_half(n4_l, h)))
            else:
                nc.scalar.activation(g4[m][:, half(h)], st_win[m][:].indirect(list_half(n4_l, h)), ACT.Copy)

        def finish(m, cols):
            nc.vector.tensor_tensor(res[m][:, cols], st_win[m][:, cols], g4[m][:, cols], ALU.max)
            nc.sync.dma_start(out[block(m), cols], res[m][:, cols])

        whole = slice(0, H)
        wa_bf0 = cast_weight("wa_bf0", wa_raw[0][:], HALF)
        wa_bf1 = cast_weight("wa_bf1", wa_raw[1][:], HALF, "gpsimd")
        for t in range(4):
            empty_b(t, "vector")
            fetch1(t)
        turn_gains("vector")
        quantize_wa(0, wa_bf0)
        a_chunk(0)
        fetch2(0)
        quantize_wa(1, wa_bf1)
        a_chunk(1)
        for t in range(1, 4):
            fetch2(t)
        for t in range(4):
            z2_row(t, "scalar")
        tanh(0, 0, 2)
        tanh(0, 2, 4)
        z2_bf0 = weave("z2_bf0", z2_rows[:, :, half(0)], HALF)
        z2_bf1 = weave("z2_bf1", z2_rows[:, :, half(1)], HALF, "scalar")
        for t in range(4):
            z_row(0, t)
        weave_z(0)
        quantize_z2(0, z2_bf0)
        quantize_z2(1, z2_bf1)
        moment(0)
        tanh(1, 0, 2)
        tanh(1, 2, 4)
        weave_z(1)
        for t in range(4):
            z_row(1, t)
        moment(1)
        empty_cv(0, "scalar")
        empty_cv(1, "scalar")
        fetch3(0)
        fetch3(1)
        weave_z(2)
        weave_z(3)
        moment(2)
        moment(3)
        diff3(0, whole)
        empty_cv(2, "vector")
        fetch3(2)
        empty_cv(3, "vector")
        diff3(1, whole)
        fetch3(3)
        fetch4(0, "vector")
        diff3(2, whole)
        fetch4(1)
        finish(0, whole)
        diff3(3, whole)
        fetch4(2)
        finish(1, whole)
        fetch4_half("vector", 3, 0)
        fetch4_half("scalar", 3, 1)
        finish(2, whole)
        finish(3, half(0))
        finish(3, half(1))
